import numpy as np
import ml_dtypes


def mxq(x, axis, fmt="e4m3"):
    dtype, down = {"e4m3": (ml_dtypes.float8_e4m3fn, 7), "e5m2": (ml_dtypes.float8_e5m2, 14)}[fmt]
    v = np.moveaxis(np.asarray(x, np.float32).astype(ml_dtypes.bfloat16).astype(np.float64), axis, -1)
    blocks = v.reshape(v.shape[:-1] + (-1, 32))
    amax = np.abs(blocks).max(-1, keepdims=True)
    byte = np.maximum(np.where(amax > 0, np.frexp(amax)[1] - 1 + 127, 0) - down, 1)
    scale = np.exp2(byte - 127.0)
    codes = (blocks / scale).astype(np.float32).astype(dtype).astype(np.float64)
    return np.moveaxis((codes * scale).reshape(v.shape), -1, axis)


WIDE = False


def mx_kscale(k):
    if not WIDE:
        return np.ones(k)
    levels = np.array([10, -10, 5, -5, 0])
    if k % 512:
        return np.exp2(np.random.permutation(np.resize(levels, k // 32))).repeat(32)
    a = np.empty((k // 512, 16))
    for p in range(k // 512):
        a[p, :8] = np.random.permutation(np.resize(levels, 8))
        for g in range(8):
            far = levels[np.abs(levels - a[p, g]) >= 10]
            a[p, g + 8] = far[np.random.randint(len(far))]
    return np.exp2(a.ravel()).repeat(32)


def f64(x):
    return np.asarray(x).astype(np.float64)


def striped(idx):
    return np.tile(idx.reshape(-1, 16).T, (8, 1)).astype(np.uint16)


def unstriped(offs):
    return offs[:16].T.reshape(-1).astype(np.int64)


E2M1 = np.array([0.0, 0.5, 1.0, 1.5, 2.0, 3.0, 4.0, 6.0, -0.0, -0.5, -1.0, -1.5, -2.0, -3.0, -4.0, -6.0])


def pack_fp4(w):
    k, n = w.shape
    w = f64(np.asarray(w, np.float32).astype(ml_dtypes.bfloat16)).reshape(k // 32, 32, n)
    amax = np.abs(w).max(1)
    mant, ex = np.frexp(amax / 6.0)
    byte = np.clip(np.where(amax > 0, np.where(mant > 0.5, ex, ex - 1) + 127, 1), 1, 254)
    scaled = (w * np.exp2(127.0 - byte)[:, None, :]).reshape(k, n).astype(np.float32)
    c = np.ascontiguousarray(scaled.reshape(k // 512, 128, 4, n).transpose(0, 1, 3, 2)).astype(ml_dtypes.float4_e2m1fn).view(np.uint8) & 0xF
    words = (c[..., 0::2] | (c[..., 1::2] << 4)).reshape(k // 512, 128, 2 * n)
    return np.ascontiguousarray(words), np.ascontiguousarray(byte.astype(np.uint8).reshape(k // 512, 16, n))


def unpack_fp4(words, scales):
    g, _, n = scales.shape
    words = np.ascontiguousarray(words).reshape(g, 128, n, 2)
    nib = np.empty((g, 128, n, 4), np.uint8)
    nib[..., 0::2] = words & 0xF
    nib[..., 1::2] = words >> 4
    vals = E2M1[nib] * np.repeat(np.exp2(scales.astype(np.float64) - 127.0), 8, axis=1)[..., None]
    return vals.transpose(0, 1, 3, 2).reshape(g * 512, n)


K, T, S, N = 1024, 2048, 1024, 128
P = 2 ** 7


def setup_inputs():
    n = np.random.standard_normal
    s = mx_kscale(K)[:, None]
    packed_w1 = pack_fp4(n((K, N)) / np.sqrt(K) / s)
    return {
        "xT": (n((K, T)) * s).astype(np.float32),
        "gate": np.tile(np.random.uniform(0.2, 1.0, T), (P, 1)).astype(np.float32),
        "w1_words": packed_w1[0],
        "w1_scales": packed_w1[1],
        "offs": striped(np.random.permutation(T)[:S]),
    }


def reference(xT, gate, w1_words, w1_scales, offs):
    xq = mxq(f64(xT)[:, unstriped(offs)], 0, "e4m3")
    y = unpack_fp4(w1_words, w1_scales).T @ xq
    g = f64(gate)[:1][:, unstriped(offs)]
    out = np.zeros((N, T))
    out[:, unstriped(offs)] = y * g
    return out

@@ -1,0 +1,148 @@
+from contextlib import ExitStack
+
+import concourse.mybir as mybir
+from concourse.masks import make_identity
+
+K, T, S, M = 1024, 2048, 1024, 128
+FLOPS = 2 * K * S * M
+
+F32 = mybir.dt.float32
+BF16 = mybir.dt.bfloat16
+I32 = mybir.dt.int32
+U32 = mybir.dt.uint32
+U16 = mybir.dt.uint16
+U8 = mybir.dt.uint8
+FP8X4 = mybir.dt.float8_e4m3fn_x4
+FP4X4 = mybir.dt.float4_e2m1fn_x4
+MULT = mybir.AluOpType.mult
+
+P = 128
+PACK = 4
+K_PASS = P * PACK
+PASSES = K // K_PASS
+STRIPE = 16
+RUN = T // P
+PER_BANK = 4
+CHUNK = 256
+N_TILE = 128
+LOAD_WIDTHS = [1024, 1024]
+LAST_LOAD_WIDTHS = [1024, 512, 512]
+VECTOR_SHARE = 4
+
+
+def tile_picked_modgate_linnone_l_kernel(tc, xT, gate, w1_words, w1_scales, offs, out):
+    nc = tc.nc
+    with ExitStack() as ctx:
+        keep = ctx.enter_context(tc.tile_pool(name="keep", bufs=1))
+        psum = ctx.enter_context(tc.psum_pool(name="psum", bufs=1))
+
+        offsets = keep.tile([P, S // STRIPE], U16, name="offsets")
+        nc.sync.dma_start(offsets[:], offs)
+
+        def entries(lo, hi):
+            return offsets[:, lo // STRIPE : hi // STRIPE]
+
+        gate_runs = keep.tile([P, RUN], F32, name="gate_runs")
+        nc.sync.dma_start(gate_runs[:], gate[0].rearrange("(p c) -> p c", c=RUN))
+
+        raw = {}
+        for g in range(PASSES):
+            rows = xT[g * K_PASS : (g + 1) * K_PASS, :].rearrange("(p j) t -> p j t", j=PACK)
+            for u in range(2):
+                widths = LAST_LOAD_WIDTHS if (g, u) == (PASSES - 1, 1) else LOAD_WIDTHS
+                raw[g, u] = []
+                c0 = 0
+                for width in widths:
+                    piece = keep.tile([P, 2, width], F32, name="raw_%d_%d_%d" % (g, u, c0))
+                    nc.sync.dma_start(piece[:], rows[:, 2 * u : 2 * u + 2, c0 : c0 + width])
+                    raw[g, u].append((piece, c0, width))
+                    c0 = c0 + width
+
+        w_words = keep.tile([P, PASSES, 2 * M], U8, name="w_words", align_bytes=64)
+        w_scales = keep.tile([P, PASSES, M], U8, name="w_scales", align_bytes=64)
+        nc.vector.memset(w_scales[:].bitcast(I32), 0)
+        nc.scalar.dma_start(w_words[:].bitcast(I32), w1_words.rearrange("g p b -> p g b").bitcast(I32))
+        for q in range(4):
+            nc.scalar.dma_start(
+                w_scales[32 * q : 32 * q + 4].bitcast(I32),
+                w1_scales[:, 4 * q : 4 * q + 4, :].rearrange("g r c -> r g c").bitcast(I32),
+            )
+
+        placed = keep.tile([P, T], F32, name="placed")
+        nc.vector.memset(placed[:], 0.0)
+
+        identity = keep.tile([P, P], F32, name="identity")
+        make_identity(nc, identity[:])
+        gate_all = keep.tile([P, T], F32, name="gate_all")
+        gate_by_bank = gate_all[:].rearrange("m (p b i) -> m p b i", b=RUN // PER_BANK, i=PER_BANK)
+        for b in range(RUN // PER_BANK):
+            spread = psum.tile([P, PER_BANK, P], F32, name="spread_%d" % b)
+            for i in range(PER_BANK):
+                c = PER_BANK * b + i
+                nc.tensor.transpose(spread[:, i, :], gate_runs[:, c : c + 1].to_broadcast([P, P]), identity[:])
+            nc.vector.tensor_copy(gate_by_bank[:, :, b, :], spread[:].rearrange("m i p -> m p i"))
+        gate_picked = keep.tile([P, S], F32, name="gate_picked")
+        nc.vector.tensor_copy(gate_picked[:], gate_all[:].indirect(offsets[:]))
+
+        def cast_pair(g, u):
+            pairs = keep.tile([P, T], U32, name="pairs_%d_%d" % (g, u))
+            for n, (piece, c0, width) in enumerate(raw[g, u]):
+                last = (g, u) == (PASSES - 1, 1) and n == len(raw[g, u]) - 1
+                cut = width // 2 if last else width - width // VECTOR_SHARE
+                for copy, lo, hi in ((nc.scalar.copy, 0, cut), (nc.vector.tensor_copy, cut, width)):
+                    copy(
+                        pairs[:, c0 + lo : c0 + hi].bitcast(BF16).rearrange("p (c e) -> p c e", e=2),
+                        piece[:, :, lo:hi].rearrange("p e c -> p c e"),
+                    )
+            return pairs
+
+        def weave(picked, lo, hi, name):
+            woven = keep.tile([P, hi - lo, 2], U32, name=name, align_bytes=64)
+            nc.scalar.copy(woven[:], picked[:, :, lo:hi].rearrange("p u j -> p j u"))
+            return woven
+
+        codes = [keep.tile([P, S], U32, name="codes_%d" % g, align_bytes=64) for g in range(PASSES)]
+        scales = [keep.tile([P, S], U8, name="scales_%d" % g, align_bytes=64) for g in range(PASSES)]
+
+        def quantize(g, woven, lo, hi):
+            nc.vector.quantize_mx(
+                out=codes[g][:, lo:hi].bitcast(FP8X4),
+                scales=scales[g][:, lo:hi],
+                in_=woven[:].rearrange("p j u -> p (j u)").bitcast(BF16),
+            )
+
+        picked_first = keep.tile([P, 2, S], U32, name="picked_first")
+        for u in range(2):
+            pairs = cast_pair(0, u)
+            nc.vector.tensor_copy(picked_first[:, u, :], pairs[:].indirect(offsets[:]))
+
+        chunks = [(lo, lo + CHUNK) for lo in range(0, S, CHUNK)]
+        picked_last = [keep.tile([P, 2, CHUNK], U32, name="picked_last_%d" % lo) for lo, hi in chunks]
+        pairs = cast_pair(1, 0)
+        for lo in range(0, S, S // 2):
+            quantize(0, weave(picked_first, lo, lo + S // 2, "woven_first_%d" % lo), lo, lo + S // 2)
+        for picked, (lo, hi) in zip(picked_last, chunks):
+            nc.vector.tensor_copy(picked[:, 0, :], pairs[:].indirect(entries(lo, hi)))
+        pairs = cast_pair(1, 1)
+        for picked, (lo, hi) in zip(picked_last, chunks):
+            nc.vector.tensor_copy(picked[:, 1, :], pairs[:].indirect(entries(lo, hi)))
+
+        y = keep.tile([P, S], F32, name="y")
+        for picked, (lo, hi) in zip(picked_last, chunks):
+            quantize(1, weave(picked, 0, CHUNK, "woven_last_%d" % lo), lo, hi)
+            acc = psum.tile([P, CHUNK], F32, name="acc_%d" % lo)
+            for n0 in range(lo, hi, N_TILE):
+                for g in range(PASSES):
+                    nc.tensor.matmul_mx(
+                        out=acc[:, n0 - lo : n0 - lo + N_TILE],
+                        lhsT=w_words[:, g, :].bitcast(FP4X4),
+                        lhsT_scale=w_scales[:, g, :],
+                        rhs=codes[g][:, n0 : n0 + N_TILE].bitcast(FP8X4),
+                        rhs_scale=scales[g][:, n0 : n0 + N_TILE],
+                        start=(g == 0),
+                        stop=(g == PASSES - 1),
+                    )
+            nc.scalar.copy(y[:, lo:hi], acc[:])
+        for lo, hi in chunks:
+            nc.vector.tensor_tensor(placed[:].indirect(entries(lo, hi)), y[:, lo:hi], gate_picked[:, lo:hi], MULT)
+        nc.sync.dma_start(out, placed[:])

@@ -25,15 +25,16 @@ RUN = T // P
 PER_BANK = 4
 CHUNK = 256
 N_TILE = 128
-LOAD_WIDTHS = [1024, 1024]
-LAST_LOAD_WIDTHS = [1024, 512, 512]
-VECTOR_SHARE = 4
+LOAD_WIDTHS = {(0, 0): [768, 768, 512], (0, 1): [1024, 1024], (1, 0): [1024, 1024], (1, 1): [1024, 512, 512]}
+VECTOR_COLUMNS = {(0, 0): [0, 0, 0], (0, 1): [0, 640], (1, 0): [0, 640], (1, 1): [0, 512, 320]}
+SCATTER_CUTS = [0, 256, S]
 
 
 def tile_picked_modgate_linnone_l_kernel(tc, xT, gate, w1_words, w1_scales, offs, out):
     nc = tc.nc
     with ExitStack() as ctx:
         keep = ctx.enter_context(tc.tile_pool(name="keep", bufs=1))
+        shared = ctx.enter_context(tc.tile_pool(name="shared", bufs=1))
         psum = ctx.enter_context(tc.psum_pool(name="psum", bufs=1))
 
         offsets = keep.tile([P, S // STRIPE], U16, name="offsets")
@@ -49,11 +50,10 @@ def tile_picked_modgate_linnone_l_kernel(tc, xT, gate, w1_words, w1_scales, offs
         for g in range(PASSES):
             rows = xT[g * K_PASS : (g + 1) * K_PASS, :].rearrange("(p j) t -> p j t", j=PACK)
             for u in range(2):
-                widths = LAST_LOAD_WIDTHS if (g, u) == (PASSES - 1, 1) else LOAD_WIDTHS
                 raw[g, u] = []
                 c0 = 0
-                for width in widths:
-                    piece = keep.tile([P, 2, width], F32, name="raw_%d_%d_%d" % (g, u, c0))
+                for width in LOAD_WIDTHS[g, u]:
+                    piece = keep.tile([P, 2, width], F32, name="raw_%d_%d_%d" % (g, u, c0), align_bytes=64)
                     nc.sync.dma_start(piece[:], rows[:, 2 * u : 2 * u + 2, c0 : c0 + width])
                     raw[g, u].append((piece, c0, width))
                     c0 = c0 + width
@@ -61,9 +61,9 @@ def tile_picked_modgate_linnone_l_kernel(tc, xT, gate, w1_words, w1_scales, offs
         w_words = keep.tile([P, PASSES, 2 * M], U8, name="w_words", align_bytes=64)
         w_scales = keep.tile([P, PASSES, M], U8, name="w_scales", align_bytes=64)
         nc.vector.memset(w_scales[:].bitcast(I32), 0)
-        nc.scalar.dma_start(w_words[:].bitcast(I32), w1_words.rearrange("g p b -> p g b").bitcast(I32))
+        nc.sync.dma_start(w_words[:].bitcast(I32), w1_words.rearrange("g p b -> p g b").bitcast(I32))
         for q in range(4):
-            nc.scalar.dma_start(
+            nc.sync.dma_start(
                 w_scales[32 * q : 32 * q + 4].bitcast(I32),
                 w1_scales[:, 4 * q : 4 * q + 4, :].rearrange("g r c -> r g c").bitcast(I32),
             )
@@ -73,7 +73,7 @@ def tile_picked_modgate_linnone_l_kernel(tc, xT, gate, w1_words, w1_scales, offs
 
         identity = keep.tile([P, P], F32, name="identity")
         make_identity(nc, identity[:])
-        gate_all = keep.tile([P, T], F32, name="gate_all")
+        gate_all = shared.tile([P, T], F32, name="gate_all", offset=2 * T)
         gate_by_bank = gate_all[:].rearrange("m (p b i) -> m p b i", b=RUN // PER_BANK, i=PER_BANK)
         for b in range(RUN // PER_BANK):
             spread = psum.tile([P, PER_BANK, P], F32, name="spread_%d" % b)
@@ -85,20 +85,23 @@ def tile_picked_modgate_linnone_l_kernel(tc, xT, gate, w1_words, w1_scales, offs
         nc.vector.tensor_copy(gate_picked[:], gate_all[:].indirect(offsets[:]))
 
         def cast_pair(g, u):
-            pairs = keep.tile([P, T], U32, name="pairs_%d_%d" % (g, u))
-            for n, (piece, c0, width) in enumerate(raw[g, u]):
-                last = (g, u) == (PASSES - 1, 1) and n == len(raw[g, u]) - 1
-                cut = width // 2 if last else width - width // VECTOR_SHARE
-                for copy, lo, hi in ((nc.scalar.copy, 0, cut), (nc.vector.tensor_copy, cut, width)):
+            if (g, u) == (0, 1):
+                pairs = shared.tile([P, T], U32, name="pairs_0_1", offset=4 * T)
+            else:
+                pairs = keep.tile([P, T], U32, name="pairs_%d_%d" % (g, u))
+            for (piece, c0, width), share in zip(raw[g, u], VECTOR_COLUMNS[g, u]):
+                cut = width - share
+                shares = ((nc.scalar.copy, 0, cut), (nc.vector.tensor_copy, cut, width))
+                for copy, lo, hi in [part for part in shares if part[1] < part[2]]:
                     copy(
                         pairs[:, c0 + lo : c0 + hi].bitcast(BF16).rearrange("p (c e) -> p c e", e=2),
                         piece[:, :, lo:hi].rearrange("p e c -> p c e"),
                     )
             return pairs
 
-        def weave(picked, lo, hi, name):
-            woven = keep.tile([P, hi - lo, 2], U32, name=name, align_bytes=64)
-            nc.scalar.copy(woven[:], picked[:, :, lo:hi].rearrange("p u j -> p j u"))
+        def weave(copy, words, picked, name, tag):
+            woven = keep.tile([P, picked.shape[2], 2], U32, name=name, tag=tag, align_bytes=64)
+            copy(woven[:].bitcast(words), picked.bitcast(words).rearrange("p u j -> p j u"))
             return woven
 
         codes = [keep.tile([P, S], U32, name="codes_%d" % g, align_bytes=64) for g in range(PASSES)]
@@ -111,25 +114,32 @@ def tile_picked_modgate_linnone_l_kernel(tc, xT, gate, w1_words, w1_scales, offs
                 in_=woven[:].rearrange("p j u -> p (j u)").bitcast(BF16),
             )
 
-        picked_first = keep.tile([P, 2, S], U32, name="picked_first")
+        picked_first = shared.tile([P, 2, S], U32, name="picked_first", offset=0)
         for u in range(2):
             pairs = cast_pair(0, u)
             nc.vector.tensor_copy(picked_first[:, u, :], pairs[:].indirect(offsets[:]))
 
         chunks = [(lo, lo + CHUNK) for lo in range(0, S, CHUNK)]
-        picked_last = [keep.tile([P, 2, CHUNK], U32, name="picked_last_%d" % lo) for lo, hi in chunks]
+        picked_last = keep.tile([P, len(chunks), 2, CHUNK], U32, name="picked_last")
         pairs = cast_pair(1, 0)
-        for lo in range(0, S, S // 2):
-            quantize(0, weave(picked_first, lo, lo + S // 2, "woven_first_%d" % lo), lo, lo + S // 2)
-        for picked, (lo, hi) in zip(picked_last, chunks):
-            nc.vector.tensor_copy(picked[:, 0, :], pairs[:].indirect(entries(lo, hi)))
+        halves = (
+            (nc.vector.tensor_copy, I32, 0, S // 2, "woven_first_0"),
+            (nc.scalar.copy, U32, S // 2, S, "raw_1_0_1024"),
+        )
+        woven_first = [
+            weave(copy, words, picked_first[:, :, lo:hi], "woven_first_%d" % lo, tag) for copy, words, lo, hi, tag in halves
+        ]
+        nc.vector.tensor_copy(picked_last[:, :, 0, :], pairs[:].indirect(offsets[:]))
+        for woven, (copy, words, lo, hi, tag) in zip(woven_first, halves):
+            quantize(0, woven, lo, hi)
         pairs = cast_pair(1, 1)
-        for picked, (lo, hi) in zip(picked_last, chunks):
-            nc.vector.tensor_copy(picked[:, 1, :], pairs[:].indirect(entries(lo, hi)))
+        for c, (lo, hi) in enumerate(chunks):
+            nc.vector.tensor_copy(picked_last[:, c, 1, :], pairs[:].indirect(entries(lo, hi)))
 
         y = keep.tile([P, S], F32, name="y")
-        for picked, (lo, hi) in zip(picked_last, chunks):
-            quantize(1, weave(picked, 0, CHUNK, "woven_last_%d" % lo), lo, hi)
+        for c, (lo, hi) in enumerate(chunks):
+            name = "woven_last_%d" % lo
+            quantize(1, weave(nc.scalar.copy, U32, picked_last[:, c], name, name), lo, hi)
             acc = psum.tile([P, CHUNK], F32, name="acc_%d" % lo)
             for n0 in range(lo, hi, N_TILE):
                 for g in range(PASSES):
@@ -143,6 +153,6 @@ def tile_picked_modgate_linnone_l_kernel(tc, xT, gate, w1_words, w1_scales, offs
                         stop=(g == PASSES - 1),
                     )
             nc.scalar.copy(y[:, lo:hi], acc[:])
-        for lo, hi in chunks:
+        for lo, hi in zip(SCATTER_CUTS, SCATTER_CUTS[1:]):
             nc.vector.tensor_tensor(placed[:].indirect(entries(lo, hi)), y[:, lo:hi], gate_picked[:, lo:hi], MULT)
         nc.sync.dma_start(out, placed[:])

from contextlib import ExitStack

import concourse.mybir as mybir
from concourse.masks import make_identity

K, T, S, M = 1024, 2048, 1024, 128
FLOPS = 2 * K * S * M

F32 = mybir.dt.float32
BF16 = mybir.dt.bfloat16
I32 = mybir.dt.int32
U32 = mybir.dt.uint32
U16 = mybir.dt.uint16
U8 = mybir.dt.uint8
FP8X4 = mybir.dt.float8_e4m3fn_x4
FP4X4 = mybir.dt.float4_e2m1fn_x4
MULT = mybir.AluOpType.mult

P = 128
PACK = 4
K_PASS = P * PACK
PASSES = K // K_PASS
STRIPE = 16
RUN = T // P
PER_BANK = 4
CHUNK = 256
N_TILE = 128
LOAD_WIDTHS = {(0, 0): [768, 768, 512], (0, 1): [1024, 1024], (1, 0): [1024, 1024], (1, 1): [1024, 512, 512]}
VECTOR_COLUMNS = {(0, 0): [0, 0, 0], (0, 1): [0, 640], (1, 0): [0, 640], (1, 1): [0, 512, 320]}
SCATTER_CUTS = [0, 256, S]


def tile_picked_modgate_linnone_l_kernel(tc, xT, gate, w1_words, w1_scales, offs, out):
    nc = tc.nc
    with ExitStack() as ctx:
        keep = ctx.enter_context(tc.tile_pool(name="keep", bufs=1))
        shared = ctx.enter_context(tc.tile_pool(name="shared", bufs=1))
        psum = ctx.enter_context(tc.psum_pool(name="psum", bufs=1))

        offsets = keep.tile([P, S // STRIPE], U16, name="offsets")
        nc.sync.dma_start(offsets[:], offs)

        def entries(lo, hi):
            return offsets[:, lo // STRIPE : hi // STRIPE]

        gate_runs = keep.tile([P, RUN], F32, name="gate_runs")
        nc.sync.dma_start(gate_runs[:], gate[0].rearrange("(p c) -> p c", c=RUN))

        raw = {}
        for g in range(PASSES):
            rows = xT[g * K_PASS : (g + 1) * K_PASS, :].rearrange("(p j) t -> p j t", j=PACK)
            for u in range(2):
                raw[g, u] = []
                c0 = 0
                for width in LOAD_WIDTHS[g, u]:
                    piece = keep.tile([P, 2, width], F32, name="raw_%d_%d_%d" % (g, u, c0), align_bytes=64)
                    nc.sync.dma_start(piece[:], rows[:, 2 * u : 2 * u + 2, c0 : c0 + width])
                    raw[g, u].append((piece, c0, width))
                    c0 = c0 + width

        w_words = keep.tile([P, PASSES, 2 * M], U8, name="w_words", align_bytes=64)
        w_scales = keep.tile([P, PASSES, M], U8, name="w_scales", align_bytes=64)
        nc.vector.memset(w_scales[:].bitcast(I32), 0)
        nc.sync.dma_start(w_words[:].bitcast(I32), w1_words.rearrange("g p b -> p g b").bitcast(I32))
        for q in range(4):
            nc.sync.dma_start(
                w_scales[32 * q : 32 * q + 4].bitcast(I32),
                w1_scales[:, 4 * q : 4 * q + 4, :].rearrange("g r c -> r g c").bitcast(I32),
            )

        placed = keep.tile([P, T], F32, name="placed")
        nc.vector.memset(placed[:], 0.0)

        identity = keep.tile([P, P], F32, name="identity")
        make_identity(nc, identity[:])
        gate_all = shared.tile([P, T], F32, name="gate_all", offset=2 * T)
        gate_by_bank = gate_all[:].rearrange("m (p b i) -> m p b i", b=RUN // PER_BANK, i=PER_BANK)
        for b in range(RUN // PER_BANK):
            spread = psum.tile([P, PER_BANK, P], F32, name="spread_%d" % b)
            for i in range(PER_BANK):
                c = PER_BANK * b + i
                nc.tensor.transpose(spread[:, i, :], gate_runs[:, c : c + 1].to_broadcast([P, P]), identity[:])
            nc.vector.tensor_copy(gate_by_bank[:, :, b, :], spread[:].rearrange("m i p -> m p i"))
        gate_picked = keep.tile([P, S], F32, name="gate_picked")
        nc.vector.tensor_copy(gate_picked[:], gate_all[:].indirect(offsets[:]))

        def cast_pair(g, u):
            if (g, u) == (0, 1):
                pairs = shared.tile([P, T], U32, name="pairs_0_1", offset=4 * T)
            else:
                pairs = keep.tile([P, T], U32, name="pairs_%d_%d" % (g, u))
            for (piece, c0, width), share in zip(raw[g, u], VECTOR_COLUMNS[g, u]):
                cut = width - share
                shares = ((nc.scalar.copy, 0, cut), (nc.vector.tensor_copy, cut, width))
                for copy, lo, hi in [part for part in shares if part[1] < part[2]]:
                    copy(
                        pairs[:, c0 + lo : c0 + hi].bitcast(BF16).rearrange("p (c e) -> p c e", e=2),
                        piece[:, :, lo:hi].rearrange("p e c -> p c e"),
                    )
            return pairs

        def weave(copy, words, picked, name, tag):
            woven = keep.tile([P, picked.shape[2], 2], U32, name=name, tag=tag, align_bytes=64)
            copy(woven[:].bitcast(words), picked.bitcast(words).rearrange("p u j -> p j u"))
            return woven

        codes = [keep.tile([P, S], U32, name="codes_%d" % g, align_bytes=64) for g in range(PASSES)]
        scales = [keep.tile([P, S], U8, name="scales_%d" % g, align_bytes=64) for g in range(PASSES)]

        def quantize(g, woven, lo, hi):
            nc.vector.quantize_mx(
                out=codes[g][:, lo:hi].bitcast(FP8X4),
                scales=scales[g][:, lo:hi],
                in_=woven[:].rearrange("p j u -> p (j u)").bitcast(BF16),
            )

        picked_first = shared.tile([P, 2, S], U32, name="picked_first", offset=0)
        for u in range(2):
            pairs = cast_pair(0, u)
            nc.vector.tensor_copy(picked_first[:, u, :], pairs[:].indirect(offsets[:]))

        chunks = [(lo, lo + CHUNK) for lo in range(0, S, CHUNK)]
        picked_last = keep.tile([P, len(chunks), 2, CHUNK], U32, name="picked_last")
        pairs = cast_pair(1, 0)
        halves = (
            (nc.vector.tensor_copy, I32, 0, S // 2, "woven_first_0"),
            (nc.scalar.copy, U32, S // 2, S, "raw_1_0_1024"),
        )
        woven_first = [
            weave(copy, words, picked_first[:, :, lo:hi], "woven_first_%d" % lo, tag) for copy, words, lo, hi, tag in halves
        ]
        nc.vector.tensor_copy(picked_last[:, :, 0, :], pairs[:].indirect(offsets[:]))
        for woven, (copy, words, lo, hi, tag) in zip(woven_first, halves):
            quantize(0, woven, lo, hi)
        pairs = cast_pair(1, 1)
        for c, (lo, hi) in enumerate(chunks):
            nc.vector.tensor_copy(picked_last[:, c, 1, :], pairs[:].indirect(entries(lo, hi)))

        y = keep.tile([P, S], F32, name="y")
        for c, (lo, hi) in enumerate(chunks):
            name = "woven_last_%d" % lo
            quantize(1, weave(nc.scalar.copy, U32, picked_last[:, c], name, name), lo, hi)
            acc = psum.tile([P, CHUNK], F32, name="acc_%d" % lo)
            for n0 in range(lo, hi, N_TILE):
                for g in range(PASSES):
                    nc.tensor.matmul_mx(
                        out=acc[:, n0 - lo : n0 - lo + N_TILE],
                        lhsT=w_words[:, g, :].bitcast(FP4X4),
                        lhsT_scale=w_scales[:, g, :],
                        rhs=codes[g][:, n0 : n0 + N_TILE].bitcast(FP8X4),
                        rhs_scale=scales[g][:, n0 : n0 + N_TILE],
                        start=(g == 0),
                        stop=(g == PASSES - 1),
                    )
            nc.scalar.copy(y[:, lo:hi], acc[:])
        for lo, hi in zip(SCATTER_CUTS, SCATTER_CUTS[1:]):
            nc.vector.tensor_tensor(placed[:].indirect(entries(lo, hi)), y[:, lo:hi], gate_picked[:, lo:hi], MULT)
        nc.sync.dma_start(out, placed[:])
